import numpy as np
import ml_dtypes


def mxq(x, axis, fmt="e4m3"):
    dtype, down = {"e4m3": (ml_dtypes.float8_e4m3fn, 7), "e5m2": (ml_dtypes.float8_e5m2, 14)}[fmt]
    v = np.moveaxis(np.asarray(x, np.float32).astype(ml_dtypes.bfloat16).astype(np.float64), axis, -1)
    blocks = v.reshape(v.shape[:-1] + (-1, 32))
    amax = np.abs(blocks).max(-1, keepdims=True)
    byte = np.maximum(np.where(amax > 0, np.frexp(amax)[1] - 1 + 127, 0) - down, 1)
    scale = np.exp2(byte - 127.0)
    codes = (blocks / scale).astype(np.float32).astype(dtype).astype(np.float64)
    return np.moveaxis((codes * scale).reshape(v.shape), -1, axis)


WIDE = False


def mx_kscale(k):
    if not WIDE:
        return np.ones(k)
    levels = np.array([10, -10, 5, -5, 0])
    if k % 512:
        return np.exp2(np.random.permutation(np.resize(levels, k // 32))).repeat(32)
    a = np.empty((k // 512, 16))
    for p in range(k // 512):
        a[p, :8] = np.random.permutation(np.resize(levels, 8))
        for g in range(8):
            far = levels[np.abs(levels - a[p, g]) >= 10]
            a[p, g + 8] = far[np.random.randint(len(far))]
    return np.exp2(a.ravel()).repeat(32)


def f64(x):
    return np.asarray(x).astype(np.float64)


def striped(idx):
    return np.tile(idx.reshape(-1, 16).T, (8, 1)).astype(np.uint16)


def unstriped(offs):
    return offs[:16].T.reshape(-1).astype(np.int64)


def striped8(idx):
    return np.concatenate([x.reshape(-1, 16).T for x in idx]).astype(np.uint16)


def runs(offs, k):
    lists = np.stack([offs[16 * r : 16 * r + 16].T.reshape(-1) for r in range(8)]).astype(np.int64)
    return lists[np.arange(k) % 512 // 64]


def pack_weight(w):
    k, n = w.shape
    w = f64(np.asarray(w, np.float32).astype(ml_dtypes.bfloat16)).reshape(k // 32, 32, n)
    amax = np.abs(w).max(1)
    byte = np.clip(np.where(amax > 0, np.frexp(amax)[1] - 1 + 127 - 7, 1), 1, 254)
    scaled = (w * np.exp2(127.0 - byte)[:, None, :]).reshape(k, n).astype(np.float32)
    words = np.ascontiguousarray(scaled.reshape(k // 512, 128, 4, n).transpose(0, 1, 3, 2)).astype(ml_dtypes.float8_e4m3fn).view(np.uint8)
    return words, np.ascontiguousarray(byte.astype(np.uint8).reshape(k // 512, 16, n))


def unpack_weight(words, scales):
    g, p, n, _ = words.shape
    vals = np.ascontiguousarray(words).view(ml_dtypes.float8_e4m3fn).astype(np.float64) * np.repeat(np.exp2(scales.astype(np.float64) - 127.0), 8, axis=1)[..., None]
    return vals.transpose(0, 1, 3, 2).reshape(g * 512, n)


def relu(v):
    return np.maximum(v, 0.0)


K, T, S, H, U = 512, 2048, 512, 512, 1024


def setup_inputs():
    n = np.random.standard_normal
    s = mx_kscale(K)[:, None]
    u = mx_kscale(S)
    packed_xT = pack_weight(n((K, T)) * s)
    return {
        "x_words": packed_xT[0],
        "x_scales": packed_xT[1],
        "w1": (n((K, H)) / np.sqrt(K) / s).astype(np.float32),
        "ga": (np.random.uniform(0.5, 1.5, (H, 1)) * u[:, None]).astype(np.float32),
        "gb": (np.random.uniform(0.5, 1.5, (H, 1)) / u[:, None]).astype(np.float32),
        "offs": striped(np.random.permutation(T)[:S]),
        "n1": striped8(np.stack([np.random.permutation(S) for _ in range(8)])),
        "n2": striped8(np.stack([np.random.permutation(S) for _ in range(8)])),
        "n3": striped8(np.stack([np.random.permutation(U)[:S] for _ in range(8)])),
        "n4": striped8(np.stack([np.random.permutation(S) for _ in range(8)])),
        "n5": striped8(np.stack([np.random.permutation(U) for _ in range(8)])),
        "n6": striped8(np.stack([np.random.permutation(U) for _ in range(8)])),
    }


def reference(x_words, x_scales, w1, ga, gb, offs, n1, n2, n3, n4, n5, n6):
    xq = unpack_weight(x_words, x_scales)[:, unstriped(offs)]
    y = mxq(f64(w1), 0, "e4m3").T @ xq
    z = f64(ga) * (y[np.arange(H)[:, None], runs(n1, H)] - (y[np.arange(H)[:, None], runs(n2, H)]))
    nw = y - (relu(y[np.arange(H)[:, None], runs(n4, H)]))
    pg = np.zeros((H, U))
    pg[np.arange(H)[:, None], runs(n3, H)] = nw
    z2 = f64(gb) * pg
    s = 0.0625 * ((mxq(z, 0, "e4m3").T @ mxq(z2, 0, "e4m3")))
    return 0.75 * (s[np.arange(S)[:, None], runs(n5, S)] + s[np.arange(S)[:, None], runs(n6, S)]) - s

@@ -1,0 +1,253 @@
+from contextlib import ExitStack
+
+import concourse.mybir as mybir
+
+K, T, S, H, U = 512, 2048, 512, 512, 1024
+FLOPS = 2 * K * H * S + 2 * H * S * U
+
+F32 = mybir.dt.float32
+BF16 = mybir.dt.bfloat16
+I32 = mybir.dt.int32
+U32 = mybir.dt.uint32
+U16 = mybir.dt.uint16
+U8 = mybir.dt.uint8
+FP8X4 = mybir.dt.float8_e4m3fn_x4
+ADD = mybir.AluOpType.add
+SUBTRACT = mybir.AluOpType.subtract
+COPY = mybir.ActivationFunctionType.Copy
+RELU = mybir.ActivationFunctionType.Relu
+
+P = 128
+PACK = 4
+LANES = 16
+BANK = 512
+HALF = S // 2
+W_VECTOR_COLUMNS = 80
+S_SCALE = 0.0625
+PAIR_WEIGHT = 0.75
+
+
+def entries(offsets, start, count):
+    return offsets[:, start // LANES : (start + count) // LANES]
+
+
+def tile_picked_selfgappagezlap_none_p_kernel(
+    tc, x_words, x_scales, w1, ga, gb, offs, n1, n2, n3, n4, n5, n6, out
+):
+    nc = tc.nc
+    with ExitStack() as ctx:
+        keep = ctx.enter_context(tc.tile_pool(name="keep", bufs=1))
+        psum = ctx.enter_context(tc.psum_pool(name="psum", bufs=1))
+
+        def load_list(name, source):
+            tile = keep.tile(list(source.shape), U16, name=name)
+            nc.sync.dma_start(tile[:], source)
+            return tile
+
+        def bank(number):
+            return psum.tile([P, BANK], F32, name="bank%d" % number)
+
+        x_scale_table = keep.tile([P, T], U8, name="x_scale_table")
+        nc.vector.memset(x_scale_table[:].bitcast(I32), 0)
+        offs_sb = load_list("offs_sb", offs)
+        for q in range(4):
+            nc.scalar.dma_start(
+                x_scale_table[32 * q : 32 * q + 4, :].bitcast(I32),
+                x_scales[0, 4 * q : 4 * q + 4, :].bitcast(I32),
+            )
+        w_raw = keep.tile([P, PACK, H], F32, name="w_raw")
+        nc.sync.dma_start(w_raw[:], w1.rearrange("(p j) c -> p j c", j=PACK))
+        x_word_table = keep.tile([P, T], U32, name="x_word_table")
+        nc.sync.dma_start(
+            x_word_table[:].bitcast(I32), x_words[0].rearrange("p n r -> p (n r)").bitcast(I32)
+        )
+        ga_sb = keep.tile([P, PACK], F32, name="ga_sb")
+        gb_sb = keep.tile([P, PACK], F32, name="gb_sb")
+        nc.gpsimd.dma_start(gb_sb[:], gb.rearrange("(p t) o -> p (t o)", t=PACK))
+        nc.gpsimd.dma_start(ga_sb[:], ga.rearrange("(p t) o -> p (t o)", t=PACK))
+        n4_sb = load_list("n4_sb", n4)
+        n3_sb = load_list("n3_sb", n3)
+        n2_sb = load_list("n2_sb", n2)
+        n1_sb = load_list("n1_sb", n1)
+        n5_sb = load_list("n5_sb", n5)
+        n6_sb = load_list("n6_sb", n6)
+
+        pages = [keep.tile([P, U], F32, name="page%d" % t) for t in range(PACK)]
+        for page in pages:
+            nc.vector.memset(page[:], 0.0)
+
+        x_scale = keep.tile([P, S], U8, name="x_scale", align_bytes=64)
+        nc.vector.tensor_copy(x_scale[:], x_scale_table[:].indirect(offs_sb[:]))
+
+        w_bf = keep.tile([P, PACK, P, PACK], BF16, name="w_bf", align_bytes=64)
+        w_to = w_bf[:].rearrange("p t m j -> p m j t")
+        w_from = w_raw[:].rearrange("p j (m t) -> p m j t", t=PACK)
+        nc.vector.tensor_copy(w_to[:, :W_VECTOR_COLUMNS], w_from[:, :W_VECTOR_COLUMNS])
+        nc.scalar.copy(w_to[:, W_VECTOR_COLUMNS:], w_from[:, W_VECTOR_COLUMNS:])
+        w_code = keep.tile([P, H], U32, name="w_code", align_bytes=64)
+        w_scale = keep.tile([P, H], U8, name="w_scale", align_bytes=64)
+        nc.vector.quantize_mx(
+            out=w_code[:].bitcast(FP8X4), scales=w_scale[:], in_=w_bf[:].rearrange("p t m j -> p (t m j)")
+        )
+        neg_gb = keep.tile([P, PACK], F32, name="neg_gb")
+        nc.scalar.mul(neg_gb[:], gb_sb[:], -1.0)
+
+        x_code = keep.tile([P, S], U32, name="x_code", align_bytes=64)
+        halves = [slice(h * HALF, (h + 1) * HALF) for h in range(2)]
+        for h in range(2):
+            nc.vector.tensor_copy(
+                x_code[:, halves[h]], x_word_table[:].indirect(entries(offs_sb, h * HALF, HALF))
+            )
+
+        def project(acc, t, cols):
+            rows = slice(t * P, (t + 1) * P)
+            nc.tensor.matmul_mx(
+                out=acc,
+                lhsT=w_code[:, rows].bitcast(FP8X4),
+                lhsT_scale=w_scale[:, rows],
+                rhs=x_code[:, cols].bitcast(FP8X4),
+                rhs_scale=x_scale[:, cols],
+                start=True,
+                stop=True,
+            )
+
+        y_parts = []
+        first = [bank(0), bank(1)]
+        for h in range(2):
+            project(first[h][:, :HALF], 0, halves[h])
+        y_parts.append([(first[h][:, :HALF], halves[h]) for h in range(2)])
+        for t in range(1, PACK):
+            acc = bank(t + 1)
+            project(acc[:], t, slice(0, S))
+            y_parts.append([(acc[:], slice(0, S))])
+
+        y_plain = [keep.tile([P, S], F32, name="y_plain%d" % t) for t in range(PACK)]
+        y_relu = [keep.tile([P, S], F32, name="y_relu%d" % t) for t in range(PACK)]
+        y_ga = [keep.tile([P, S], F32, name="y_ga%d" % t) for t in range(PACK)]
+        neg_nw = [keep.tile([P, S], F32, name="neg_nw%d" % t) for t in range(PACK)]
+        nw_gb = [keep.tile([P, S], F32, name="nw_gb%d" % t) for t in range(PACK)]
+        z2_bf = keep.tile([P, U, PACK], BF16, name="z2_bf", align_bytes=64)
+
+        def fetch_n4(t):
+            for acc, cols in y_parts[t]:
+                nc.scalar.activation(y_relu[t][:, cols], acc, RELU)
+                nc.scalar.copy(y_plain[t][:, cols], acc)
+            for h in range(2):
+                nc.vector.tensor_tensor(
+                    neg_nw[t][:, halves[h]],
+                    y_relu[t][:].indirect(entries(n4_sb, h * HALF, HALF)),
+                    y_plain[t][:, halves[h]],
+                    SUBTRACT,
+                )
+
+        def put_n3(t):
+            nc.scalar.activation(nw_gb[t][:], neg_nw[t][:], COPY, scale=neg_gb[:, t : t + 1])
+            nc.vector.tensor_copy(pages[t][:].indirect(n3_sb[:]), nw_gb[t][:])
+
+        def round_page(t):
+            nc.scalar.copy(z2_bf[:, :, t], pages[t][:])
+
+        fetch_n4(0)
+        fetch_n4(1)
+        put_n3(0)
+        fetch_n4(2)
+        put_n3(1)
+        fetch_n4(3)
+        round_page(0)
+        put_n3(2)
+        round_page(1)
+        put_n3(3)
+        for t in range(PACK):
+            for acc, cols in y_parts[t]:
+                nc.scalar.activation(y_ga[t][:, cols], acc, COPY, scale=ga_sb[:, t : t + 1])
+        round_page(2)
+        round_page(3)
+
+        at_n2 = [keep.tile([P, PACK, HALF], F32, name="at_n2_%d" % h) for h in range(2)]
+        z = [keep.tile([P, PACK, HALF], F32, name="z%d" % h) for h in range(2)]
+        z_bf = keep.tile([P, PACK, P, PACK], BF16, name="z_bf", align_bytes=64)
+
+        def fetch_z(pieces):
+            for t, h in pieces:
+                nc.vector.tensor_copy(at_n2[h][:, t, :], y_ga[t][:].indirect(entries(n2_sb, h * HALF, HALF)))
+            for t, h in pieces:
+                nc.vector.tensor_tensor(
+                    z[h][:, t, :],
+                    y_ga[t][:].indirect(entries(n1_sb, h * HALF, HALF)),
+                    at_n2[h][:, t, :],
+                    SUBTRACT,
+                )
+
+        def round_z(h):
+            places = slice(h * HALF // PACK, (h + 1) * HALF // PACK)
+            nc.scalar.copy(
+                z_bf[:].rearrange("p i m t -> p m t i")[:, places],
+                z[h][:].rearrange("p t (m i) -> p m t i", i=PACK),
+            )
+
+        fetch_z([(0, 0), (0, 1)])
+        fetch_z([(1, 0), (1, 1)])
+        fetch_z([(2, 0), (3, 0)])
+        round_z(0)
+        fetch_z([(2, 1), (3, 1)])
+        round_z(1)
+
+        z2_code = keep.tile([P, U], U32, name="z2_code", align_bytes=64)
+        z2_scale = keep.tile([P, U], U8, name="z2_scale", align_bytes=64)
+        for b in range(2):
+            cols = slice(b * BANK, (b + 1) * BANK)
+            nc.vector.quantize_mx(
+                out=z2_code[:, cols].bitcast(FP8X4),
+                scales=z2_scale[:, cols],
+                in_=z2_bf[:, cols, :].rearrange("p w t -> p (w t)"),
+            )
+        z_code = keep.tile([P, S], U32, name="z_code", align_bytes=64)
+        z_scale = keep.tile([P, S], U8, name="z_scale", align_bytes=64)
+        out_rows = out.rearrange("(p i) w -> p i w", i=PACK)
+        s_banks = []
+        for i in range(PACK):
+            rows = slice(i * P, (i + 1) * P)
+            nc.vector.quantize_mx(
+                out=z_code[:, rows].bitcast(FP8X4),
+                scales=z_scale[:, rows],
+                in_=z_bf[:, i].rearrange("p m t -> p (m t)"),
+            )
+            s_banks.append([bank(2 * i), bank(2 * i + 1)])
+            for b in range(2):
+                cols = slice(b * BANK, (b + 1) * BANK)
+                nc.tensor.matmul_mx(
+                    out=s_banks[i][b][:],
+                    lhsT=z_code[:, rows].bitcast(FP8X4),
+                    lhsT_scale=z_scale[:, rows],
+                    rhs=z2_code[:, cols].bitcast(FP8X4),
+                    rhs_scale=z2_scale[:, cols],
+                    start=True,
+                    stop=True,
+                )
+
+        for i in range(PACK):
+            s_plain = keep.tile([P, U], F32, name="s_plain%d" % i)
+            s_pair = keep.tile([P, U], F32, name="s_pair%d" % i)
+            partial = keep.tile([P, U], F32, name="partial%d" % i)
+            result = keep.tile([P, U], F32, name="result%d" % i)
+            for target, factor in ((s_plain, S_SCALE), (s_pair, S_SCALE * PAIR_WEIGHT)):
+                for b in range(2):
+                    cols = slice(b * BANK, (b + 1) * BANK)
+                    if i == 0 and b == 1:
+                        nc.vector.tensor_scalar_mul(target[:, cols], s_banks[i][b][:], factor)
+                    else:
+                        nc.scalar.mul(target[:, cols], s_banks[i][b][:], factor)
+            for b in range(2):
+                cols = slice(b * BANK, (b + 1) * BANK)
+                nc.vector.tensor_tensor(
+                    partial[:, cols], s_pair[:].indirect(entries(n5_sb, b * BANK, BANK)), s_plain[:, cols], SUBTRACT
+                )
+            widths = [BANK, BANK] if i < PACK - 1 else [BANK, BANK // 2, BANK // 2]
+            start = 0
+            for width in widths:
+                cols = slice(start, start + width)
+                nc.vector.tensor_tensor(
+                    result[:, cols], s_pair[:].indirect(entries(n6_sb, start, width)), partial[:, cols], ADD
+                )
+                nc.sync.dma_start(out_rows[:, i, cols], result[:, cols])
+                start = start + width

@@ -22,7 +22,7 @@ PACK = 4
 LANES = 16
 BANK = 512
 HALF = S // 2
-W_VECTOR_COLUMNS = 80
+W_VECTOR_COLUMNS = 88
 S_SCALE = 0.0625
 PAIR_WEIGHT = 0.75
 
@@ -48,56 +48,70 @@ def tile_picked_selfgappagezlap_none_p_kernel(
             return psum.tile([P, BANK], F32, name="bank%d" % number)
 
         x_scale_table = keep.tile([P, T], U8, name="x_scale_table")
-        nc.vector.memset(x_scale_table[:].bitcast(I32), 0)
+        nc.gpsimd.memset(x_scale_table[:].bitcast(I32), 0)
+        w_raw = keep.tile([P, PACK, H], F32, name="w_raw", tag="w_raw", align_bytes=64)
+        nc.sync.dma_start(w_raw[:], w1.rearrange("(p j) c -> p j c", j=PACK))
         offs_sb = load_list("offs_sb", offs)
         for q in range(4):
-            nc.scalar.dma_start(
+            nc.sync.dma_start(
                 x_scale_table[32 * q : 32 * q + 4, :].bitcast(I32),
                 x_scales[0, 4 * q : 4 * q + 4, :].bitcast(I32),
             )
-        w_raw = keep.tile([P, PACK, H], F32, name="w_raw")
-        nc.sync.dma_start(w_raw[:], w1.rearrange("(p j) c -> p j c", j=PACK))
         x_word_table = keep.tile([P, T], U32, name="x_word_table")
         nc.sync.dma_start(
             x_word_table[:].bitcast(I32), x_words[0].rearrange("p n r -> p (n r)").bitcast(I32)
         )
         ga_sb = keep.tile([P, PACK], F32, name="ga_sb")
         gb_sb = keep.tile([P, PACK], F32, name="gb_sb")
-        nc.gpsimd.dma_start(gb_sb[:], gb.rearrange("(p t) o -> p (t o)", t=PACK))
-        nc.gpsimd.dma_start(ga_sb[:], ga.rearrange("(p t) o -> p (t o)", t=PACK))
         n4_sb = load_list("n4_sb", n4)
+        nc.sync.dma_start(gb_sb[:], gb.rearrange("(p t) o -> p (t o)", t=PACK))
         n3_sb = load_list("n3_sb", n3)
+        nc.sync.dma_start(ga_sb[:], ga.rearrange("(p t) o -> p (t o)", t=PACK))
         n2_sb = load_list("n2_sb", n2)
         n1_sb = load_list("n1_sb", n1)
         n5_sb = load_list("n5_sb", n5)
         n6_sb = load_list("n6_sb", n6)
 
-        pages = [keep.tile([P, U], F32, name="page%d" % t) for t in range(PACK)]
-        for page in pages:
-            nc.vector.memset(page[:], 0.0)
+        pages = []
 
-        x_scale = keep.tile([P, S], U8, name="x_scale", align_bytes=64)
-        nc.vector.tensor_copy(x_scale[:], x_scale_table[:].indirect(offs_sb[:]))
+        def clear_page(tag):
+            page = keep.tile([P, U], F32, name="page%d" % len(pages), tag=tag, align_bytes=64)
+            nc.gpsimd.memset(page[:], 0.0)
+            pages.append(page)
+
+        clear_page("page0")
+        clear_page("page1")
 
         w_bf = keep.tile([P, PACK, P, PACK], BF16, name="w_bf", align_bytes=64)
         w_to = w_bf[:].rearrange("p t m j -> p m j t")
         w_from = w_raw[:].rearrange("p j (m t) -> p m j t", t=PACK)
         nc.vector.tensor_copy(w_to[:, :W_VECTOR_COLUMNS], w_from[:, :W_VECTOR_COLUMNS])
         nc.scalar.copy(w_to[:, W_VECTOR_COLUMNS:], w_from[:, W_VECTOR_COLUMNS:])
-        w_code = keep.tile([P, H], U32, name="w_code", align_bytes=64)
-        w_scale = keep.tile([P, H], U8, name="w_scale", align_bytes=64)
-        nc.vector.quantize_mx(
-            out=w_code[:].bitcast(FP8X4), scales=w_scale[:], in_=w_bf[:].rearrange("p t m j -> p (t m j)")
-        )
+        x_scale = keep.tile([P, S], U8, name="x_scale", align_bytes=64)
+        nc.vector.tensor_copy(x_scale[:], x_scale_table[:].indirect(offs_sb[:]))
+        w_code = keep.tile([P, H], U32, name="w_code", tag="w_code", align_bytes=64)
+        w_scale = keep.tile([P, H], U8, name="w_scale", tag="w_scale", align_bytes=64)
+
+        def quantize_w(first, last):
+            cols = slice(first * P, last * P)
+            nc.vector.quantize_mx(
+                out=w_code[:, cols].bitcast(FP8X4),
+                scales=w_scale[:, cols],
+                in_=w_bf[:, first:last].rearrange("p t m j -> p (t m j)"),
+            )
+
+        quantize_w(0, 1)
         neg_gb = keep.tile([P, PACK], F32, name="neg_gb")
         nc.scalar.mul(neg_gb[:], gb_sb[:], -1.0)
 
-        x_code = keep.tile([P, S], U32, name="x_code", align_bytes=64)
+        x_code = keep.tile([P, S], U32, name="x_code", tag="w_raw", align_bytes=64)
         halves = [slice(h * HALF, (h + 1) * HALF) for h in range(2)]
         for h in range(2):
             nc.vector.tensor_copy(
                 x_code[:, halves[h]], x_word_table[:].indirect(entries(offs_sb, h * HALF, HALF))
             )
+        quantize_w(1, 2)
+        quantize_w(2, PACK)
 
         def project(acc, t, cols):
             rows = slice(t * P, (t + 1) * P)
@@ -120,6 +134,8 @@ def tile_picked_selfgappagezlap_none_p_kernel(
             acc = bank(t + 1)
             project(acc[:], t, slice(0, S))
             y_parts.append([(acc[:], slice(0, S))])
+        clear_page("w_code")
+        clear_page("w_scale")
 
         y_plain = [keep.tile([P, S], F32, name="y_plain%d" % t) for t in range(PACK)]
         y_relu = [keep.tile([P, S], F32, name="y_relu%d" % t) for t in range(PACK)]
@@ -225,29 +241,55 @@ def tile_picked_selfgappagezlap_none_p_kernel(
                     stop=True,
                 )
 
+        quarter = BANK // 2
         for i in range(PACK):
             s_plain = keep.tile([P, U], F32, name="s_plain%d" % i)
             s_pair = keep.tile([P, U], F32, name="s_pair%d" % i)
             partial = keep.tile([P, U], F32, name="partial%d" % i)
             result = keep.tile([P, U], F32, name="result%d" % i)
-            for target, factor in ((s_plain, S_SCALE), (s_pair, S_SCALE * PAIR_WEIGHT)):
-                for b in range(2):
-                    cols = slice(b * BANK, (b + 1) * BANK)
-                    if i == 0 and b == 1:
-                        nc.vector.tensor_scalar_mul(target[:, cols], s_banks[i][b][:], factor)
-                    else:
-                        nc.scalar.mul(target[:, cols], s_banks[i][b][:], factor)
-            for b in range(2):
-                cols = slice(b * BANK, (b + 1) * BANK)
-                nc.vector.tensor_tensor(
-                    partial[:, cols], s_pair[:].indirect(entries(n5_sb, b * BANK, BANK)), s_plain[:, cols], SUBTRACT
+
+            def scale_out(target, start, width, factor):
+                b = start // BANK
+                nc.scalar.mul(
+                    target[:, start : start + width],
+                    s_banks[i][b][:, start - b * BANK : start - b * BANK + width],
+                    factor,
                 )
-            widths = [BANK, BANK] if i < PACK - 1 else [BANK, BANK // 2, BANK // 2]
-            start = 0
-            for width in widths:
+
+            def fetch_n5(start, width):
+                cols = slice(start, start + width)
+                nc.vector.tensor_tensor(
+                    partial[:, cols], s_pair[:].indirect(entries(n5_sb, start, width)), s_plain[:, cols], SUBTRACT
+                )
+
+            def fetch_n6(start, width):
                 cols = slice(start, start + width)
                 nc.vector.tensor_tensor(
                     result[:, cols], s_pair[:].indirect(entries(n6_sb, start, width)), partial[:, cols], ADD
                 )
                 nc.sync.dma_start(out_rows[:, i, cols], result[:, cols])
-                start = start + width
+
+            if i == 0:
+                scale_out(s_pair, 0, BANK, S_SCALE * PAIR_WEIGHT)
+                nc.vector.tensor_scalar_mul(s_pair[:, BANK:], s_banks[i][1][:], S_SCALE * PAIR_WEIGHT)
+                scale_out(s_plain, 0, quarter, S_SCALE)
+                scale_out(s_plain, quarter, quarter, S_SCALE)
+                scale_out(s_plain, BANK, BANK, S_SCALE)
+                fetch_n5(0, quarter)
+                fetch_n5(quarter, quarter)
+                fetch_n6(0, quarter)
+                fetch_n5(BANK, BANK)
+                fetch_n6(quarter, quarter)
+                fetch_n6(BANK, BANK)
+            else:
+                for target, factor in ((s_plain, S_SCALE), (s_pair, S_SCALE * PAIR_WEIGHT)):
+                    for b in range(2):
+                        scale_out(target, b * BANK, BANK, factor)
+                for b in range(2):
+                    fetch_n5(b * BANK, BANK)
+                fetch_n6(0, BANK)
+                if i < PACK - 1:
+                    fetch_n6(BANK, BANK)
+                else:
+                    fetch_n6(BANK, quarter)
+                    fetch_n6(BANK + quarter, quarter)

@@ -22,7 +22,7 @@ PACK = 4
 LANES = 16
 BANK = 512
 HALF = S // 2
-W_VECTOR_COLUMNS = 88
+W_VECTOR_COLUMNS = 72
 S_SCALE = 0.0625
 PAIR_WEIGHT = 0.75
 
@@ -147,7 +147,11 @@ def tile_picked_selfgappagezlap_none_p_kernel(
         def fetch_n4(t):
             for acc, cols in y_parts[t]:
                 nc.scalar.activation(y_relu[t][:, cols], acc, RELU)
-                nc.scalar.copy(y_plain[t][:, cols], acc)
+                if t == 1:
+                    for h in range(2):
+                        nc.scalar.copy(y_plain[t][:, halves[h]], acc[:, halves[h]])
+                else:
+                    nc.scalar.copy(y_plain[t][:, cols], acc)
             for h in range(2):
                 nc.vector.tensor_tensor(
                     neg_nw[t][:, halves[h]],
@@ -179,44 +183,55 @@ def tile_picked_selfgappagezlap_none_p_kernel(
         round_page(2)
         round_page(3)
 
-        at_n2 = [keep.tile([P, PACK, HALF], F32, name="at_n2_%d" % h) for h in range(2)]
-        z = [keep.tile([P, PACK, HALF], F32, name="z%d" % h) for h in range(2)]
+        stretches = [(0, HALF), (HALF, HALF // 2), (HALF + HALF // 2, HALF // 2), (HALF, HALF)]
+        at_n2 = [keep.tile([P, S], F32, name="at_n2_%d" % t) for t in range(PACK)]
+        z = keep.tile([P, PACK * S], F32, name="z")
         z_bf = keep.tile([P, PACK, P, PACK], BF16, name="z_bf", align_bytes=64)
 
-        def fetch_z(pieces):
-            for t, h in pieces:
-                nc.vector.tensor_copy(at_n2[h][:, t, :], y_ga[t][:].indirect(entries(n2_sb, h * HALF, HALF)))
-            for t, h in pieces:
+        def fetch_n2(pieces):
+            for t, c in pieces:
+                start, count = stretches[c]
+                nc.vector.tensor_copy(
+                    at_n2[t][:, start : start + count], y_ga[t][:].indirect(entries(n2_sb, start, count))
+                )
+
+        def fetch_n1(pieces):
+            for t, c in pieces:
+                start, count = stretches[c]
                 nc.vector.tensor_tensor(
-                    z[h][:, t, :],
-                    y_ga[t][:].indirect(entries(n1_sb, h * HALF, HALF)),
-                    at_n2[h][:, t, :],
+                    z[:, t * S + start : t * S + start + count],
+                    y_ga[t][:].indirect(entries(n1_sb, start, count)),
+                    at_n2[t][:, start : start + count],
                     SUBTRACT,
                 )
 
-        def round_z(h):
-            places = slice(h * HALF // PACK, (h + 1) * HALF // PACK)
+        def round_z(c):
+            start, count = stretches[c]
+            places = slice(start // PACK, (start + count) // PACK)
             nc.scalar.copy(
                 z_bf[:].rearrange("p i m t -> p m t i")[:, places],
-                z[h][:].rearrange("p t (m i) -> p m t i", i=PACK),
+                z[:].rearrange("p (t m i) -> p m t i", t=PACK, i=PACK)[:, places],
             )
-
-        fetch_z([(0, 0), (0, 1)])
-        fetch_z([(1, 0), (1, 1)])
-        fetch_z([(2, 0), (3, 0)])
-        round_z(0)
-        fetch_z([(2, 1), (3, 1)])
-        round_z(1)
 
         z2_code = keep.tile([P, U], U32, name="z2_code", align_bytes=64)
         z2_scale = keep.tile([P, U], U8, name="z2_scale", align_bytes=64)
-        for b in range(2):
+
+        def quantize_z2(b):
             cols = slice(b * BANK, (b + 1) * BANK)
             nc.vector.quantize_mx(
                 out=z2_code[:, cols].bitcast(FP8X4),
                 scales=z2_scale[:, cols],
                 in_=z2_bf[:, cols, :].rearrange("p w t -> p (w t)"),
             )
+
+        for t in range(2):
+            fetch_n2([(t, c) for c in (0, 3)])
+            fetch_n1([(t, c) for c in (0, 3)])
+        for c in range(3):
+            fetch_n2([(2, c), (3, c)])
+            fetch_n1([(2, c), (3, c)])
+            round_z(c)
+        quantize_z2(0)
         z_code = keep.tile([P, S], U32, name="z_code", align_bytes=64)
         z_scale = keep.tile([P, S], U8, name="z_scale", align_bytes=64)
         out_rows = out.rearrange("(p i) w -> p i w", i=PACK)
@@ -228,6 +243,8 @@ def tile_picked_selfgappagezlap_none_p_kernel(
                 scales=z_scale[:, rows],
                 in_=z_bf[:, i].rearrange("p m t -> p (m t)"),
             )
+            if i == 0:
+                quantize_z2(1)
             s_banks.append([bank(2 * i), bank(2 * i + 1)])
             for b in range(2):
                 cols = slice(b * BANK, (b + 1) * BANK)

from contextlib import ExitStack

import concourse.mybir as mybir

K, T, S, H, U = 512, 2048, 512, 512, 1024
FLOPS = 2 * K * H * S + 2 * H * S * U

F32 = mybir.dt.float32
BF16 = mybir.dt.bfloat16
I32 = mybir.dt.int32
U32 = mybir.dt.uint32
U16 = mybir.dt.uint16
U8 = mybir.dt.uint8
FP8X4 = mybir.dt.float8_e4m3fn_x4
ADD = mybir.AluOpType.add
SUBTRACT = mybir.AluOpType.subtract
COPY = mybir.ActivationFunctionType.Copy
RELU = mybir.ActivationFunctionType.Relu

P = 128
PACK = 4
LANES = 16
BANK = 512
HALF = S // 2
W_VECTOR_COLUMNS = 72
S_SCALE = 0.0625
PAIR_WEIGHT = 0.75


def entries(offsets, start, count):
    return offsets[:, start // LANES : (start + count) // LANES]


def tile_picked_selfgappagezlap_none_p_kernel(
    tc, x_words, x_scales, w1, ga, gb, offs, n1, n2, n3, n4, n5, n6, out
):
    nc = tc.nc
    with ExitStack() as ctx:
        keep = ctx.enter_context(tc.tile_pool(name="keep", bufs=1))
        psum = ctx.enter_context(tc.psum_pool(name="psum", bufs=1))

        def load_list(name, source):
            tile = keep.tile(list(source.shape), U16, name=name)
            nc.sync.dma_start(tile[:], source)
            return tile

        def bank(number):
            return psum.tile([P, BANK], F32, name="bank%d" % number)

        x_scale_table = keep.tile([P, T], U8, name="x_scale_table")
        nc.gpsimd.memset(x_scale_table[:].bitcast(I32), 0)
        w_raw = keep.tile([P, PACK, H], F32, name="w_raw", tag="w_raw", align_bytes=64)
        nc.sync.dma_start(w_raw[:], w1.rearrange("(p j) c -> p j c", j=PACK))
        offs_sb = load_list("offs_sb", offs)
        for q in range(4):
            nc.sync.dma_start(
                x_scale_table[32 * q : 32 * q + 4, :].bitcast(I32),
                x_scales[0, 4 * q : 4 * q + 4, :].bitcast(I32),
            )
        x_word_table = keep.tile([P, T], U32, name="x_word_table")
        nc.sync.dma_start(
            x_word_table[:].bitcast(I32), x_words[0].rearrange("p n r -> p (n r)").bitcast(I32)
        )
        ga_sb = keep.tile([P, PACK], F32, name="ga_sb")
        gb_sb = keep.tile([P, PACK], F32, name="gb_sb")
        n4_sb = load_list("n4_sb", n4)
        nc.sync.dma_start(gb_sb[:], gb.rearrange("(p t) o -> p (t o)", t=PACK))
        n3_sb = load_list("n3_sb", n3)
        nc.sync.dma_start(ga_sb[:], ga.rearrange("(p t) o -> p (t o)", t=PACK))
        n2_sb = load_list("n2_sb", n2)
        n1_sb = load_list("n1_sb", n1)
        n5_sb = load_list("n5_sb", n5)
        n6_sb = load_list("n6_sb", n6)

        pages = []

        def clear_page(tag):
            page = keep.tile([P, U], F32, name="page%d" % len(pages), tag=tag, align_bytes=64)
            nc.gpsimd.memset(page[:], 0.0)
            pages.append(page)

        clear_page("page0")
        clear_page("page1")

        w_bf = keep.tile([P, PACK, P, PACK], BF16, name="w_bf", align_bytes=64)
        w_to = w_bf[:].rearrange("p t m j -> p m j t")
        w_from = w_raw[:].rearrange("p j (m t) -> p m j t", t=PACK)
        nc.vector.tensor_copy(w_to[:, :W_VECTOR_COLUMNS], w_from[:, :W_VECTOR_COLUMNS])
        nc.scalar.copy(w_to[:, W_VECTOR_COLUMNS:], w_from[:, W_VECTOR_COLUMNS:])
        x_scale = keep.tile([P, S], U8, name="x_scale", align_bytes=64)
        nc.vector.tensor_copy(x_scale[:], x_scale_table[:].indirect(offs_sb[:]))
        w_code = keep.tile([P, H], U32, name="w_code", tag="w_code", align_bytes=64)
        w_scale = keep.tile([P, H], U8, name="w_scale", tag="w_scale", align_bytes=64)

        def quantize_w(first, last):
            cols = slice(first * P, last * P)
            nc.vector.quantize_mx(
                out=w_code[:, cols].bitcast(FP8X4),
                scales=w_scale[:, cols],
                in_=w_bf[:, first:last].rearrange("p t m j -> p (t m j)"),
            )

        quantize_w(0, 1)
        neg_gb = keep.tile([P, PACK], F32, name="neg_gb")
        nc.scalar.mul(neg_gb[:], gb_sb[:], -1.0)

        x_code = keep.tile([P, S], U32, name="x_code", tag="w_raw", align_bytes=64)
        halves = [slice(h * HALF, (h + 1) * HALF) for h in range(2)]
        for h in range(2):
            nc.vector.tensor_copy(
                x_code[:, halves[h]], x_word_table[:].indirect(entries(offs_sb, h * HALF, HALF))
            )
        quantize_w(1, 2)
        quantize_w(2, PACK)

        def project(acc, t, cols):
            rows = slice(t * P, (t + 1) * P)
            nc.tensor.matmul_mx(
                out=acc,
                lhsT=w_code[:, rows].bitcast(FP8X4),
                lhsT_scale=w_scale[:, rows],
                rhs=x_code[:, cols].bitcast(FP8X4),
                rhs_scale=x_scale[:, cols],
                start=True,
                stop=True,
            )

        y_parts = []
        first = [bank(0), bank(1)]
        for h in range(2):
            project(first[h][:, :HALF], 0, halves[h])
        y_parts.append([(first[h][:, :HALF], halves[h]) for h in range(2)])
        for t in range(1, PACK):
            acc = bank(t + 1)
            project(acc[:], t, slice(0, S))
            y_parts.append([(acc[:], slice(0, S))])
        clear_page("w_code")
        clear_page("w_scale")

        y_plain = [keep.tile([P, S], F32, name="y_plain%d" % t) for t in range(PACK)]
        y_relu = [keep.tile([P, S], F32, name="y_relu%d" % t) for t in range(PACK)]
        y_ga = [keep.tile([P, S], F32, name="y_ga%d" % t) for t in range(PACK)]
        neg_nw = [keep.tile([P, S], F32, name="neg_nw%d" % t) for t in range(PACK)]
        nw_gb = [keep.tile([P, S], F32, name="nw_gb%d" % t) for t in range(PACK)]
        z2_bf = keep.tile([P, U, PACK], BF16, name="z2_bf", align_bytes=64)

        def fetch_n4(t):
            for acc, cols in y_parts[t]:
                nc.scalar.activation(y_relu[t][:, cols], acc, RELU)
                if t == 1:
                    for h in range(2):
                        nc.scalar.copy(y_plain[t][:, halves[h]], acc[:, halves[h]])
                else:
                    nc.scalar.copy(y_plain[t][:, cols], acc)
            for h in range(2):
                nc.vector.tensor_tensor(
                    neg_nw[t][:, halves[h]],
                    y_relu[t][:].indirect(entries(n4_sb, h * HALF, HALF)),
                    y_plain[t][:, halves[h]],
                    SUBTRACT,
                )

        def put_n3(t):
            nc.scalar.activation(nw_gb[t][:], neg_nw[t][:], COPY, scale=neg_gb[:, t : t + 1])
            nc.vector.tensor_copy(pages[t][:].indirect(n3_sb[:]), nw_gb[t][:])

        def round_page(t):
            nc.scalar.copy(z2_bf[:, :, t], pages[t][:])

        fetch_n4(0)
        fetch_n4(1)
        put_n3(0)
        fetch_n4(2)
        put_n3(1)
        fetch_n4(3)
        round_page(0)
        put_n3(2)
        round_page(1)
        put_n3(3)
        for t in range(PACK):
            for acc, cols in y_parts[t]:
                nc.scalar.activation(y_ga[t][:, cols], acc, COPY, scale=ga_sb[:, t : t + 1])
        round_page(2)
        round_page(3)

        stretches = [(0, HALF), (HALF, HALF // 2), (HALF + HALF // 2, HALF // 2), (HALF, HALF)]
        at_n2 = [keep.tile([P, S], F32, name="at_n2_%d" % t) for t in range(PACK)]
        z = keep.tile([P, PACK * S], F32, name="z")
        z_bf = keep.tile([P, PACK, P, PACK], BF16, name="z_bf", align_bytes=64)

        def fetch_n2(pieces):
            for t, c in pieces:
                start, count = stretches[c]
                nc.vector.tensor_copy(
                    at_n2[t][:, start : start + count], y_ga[t][:].indirect(entries(n2_sb, start, count))
                )

        def fetch_n1(pieces):
            for t, c in pieces:
                start, count = stretches[c]
                nc.vector.tensor_tensor(
                    z[:, t * S + start : t * S + start + count],
                    y_ga[t][:].indirect(entries(n1_sb, start, count)),
                    at_n2[t][:, start : start + count],
                    SUBTRACT,
                )

        def round_z(c):
            start, count = stretches[c]
            places = slice(start // PACK, (start + count) // PACK)
            nc.scalar.copy(
                z_bf[:].rearrange("p i m t -> p m t i")[:, places],
                z[:].rearrange("p (t m i) -> p m t i", t=PACK, i=PACK)[:, places],
            )

        z2_code = keep.tile([P, U], U32, name="z2_code", align_bytes=64)
        z2_scale = keep.tile([P, U], U8, name="z2_scale", align_bytes=64)

        def quantize_z2(b):
            cols = slice(b * BANK, (b + 1) * BANK)
            nc.vector.quantize_mx(
                out=z2_code[:, cols].bitcast(FP8X4),
                scales=z2_scale[:, cols],
                in_=z2_bf[:, cols, :].rearrange("p w t -> p (w t)"),
            )

        for t in range(2):
            fetch_n2([(t, c) for c in (0, 3)])
            fetch_n1([(t, c) for c in (0, 3)])
        for c in range(3):
            fetch_n2([(2, c), (3, c)])
            fetch_n1([(2, c), (3, c)])
            round_z(c)
        quantize_z2(0)
        z_code = keep.tile([P, S], U32, name="z_code", align_bytes=64)
        z_scale = keep.tile([P, S], U8, name="z_scale", align_bytes=64)
        out_rows = out.rearrange("(p i) w -> p i w", i=PACK)
        s_banks = []
        for i in range(PACK):
            rows = slice(i * P, (i + 1) * P)
            nc.vector.quantize_mx(
                out=z_code[:, rows].bitcast(FP8X4),
                scales=z_scale[:, rows],
                in_=z_bf[:, i].rearrange("p m t -> p (m t)"),
            )
            if i == 0:
                quantize_z2(1)
            s_banks.append([bank(2 * i), bank(2 * i + 1)])
            for b in range(2):
                cols = slice(b * BANK, (b + 1) * BANK)
                nc.tensor.matmul_mx(
                    out=s_banks[i][b][:],
                    lhsT=z_code[:, rows].bitcast(FP8X4),
                    lhsT_scale=z_scale[:, rows],
                    rhs=z2_code[:, cols].bitcast(FP8X4),
                    rhs_scale=z2_scale[:, cols],
                    start=True,
                    stop=True,
                )

        quarter = BANK // 2
        for i in range(PACK):
            s_plain = keep.tile([P, U], F32, name="s_plain%d" % i)
            s_pair = keep.tile([P, U], F32, name="s_pair%d" % i)
            partial = keep.tile([P, U], F32, name="partial%d" % i)
            result = keep.tile([P, U], F32, name="result%d" % i)

            def scale_out(target, start, width, factor):
                b = start // BANK
                nc.scalar.mul(
                    target[:, start : start + width],
                    s_banks[i][b][:, start - b * BANK : start - b * BANK + width],
                    factor,
                )

            def fetch_n5(start, width):
                cols = slice(start, start + width)
                nc.vector.tensor_tensor(
                    partial[:, cols], s_pair[:].indirect(entries(n5_sb, start, width)), s_plain[:, cols], SUBTRACT
                )

            def fetch_n6(start, width):
                cols = slice(start, start + width)
                nc.vector.tensor_tensor(
                    result[:, cols], s_pair[:].indirect(entries(n6_sb, start, width)), partial[:, cols], ADD
                )
                nc.sync.dma_start(out_rows[:, i, cols], result[:, cols])

            if i == 0:
                scale_out(s_pair, 0, BANK, S_SCALE * PAIR_WEIGHT)
                nc.vector.tensor_scalar_mul(s_pair[:, BANK:], s_banks[i][1][:], S_SCALE * PAIR_WEIGHT)
                scale_out(s_plain, 0, quarter, S_SCALE)
                scale_out(s_plain, quarter, quarter, S_SCALE)
                scale_out(s_plain, BANK, BANK, S_SCALE)
                fetch_n5(0, quarter)
                fetch_n5(quarter, quarter)
                fetch_n6(0, quarter)
                fetch_n5(BANK, BANK)
                fetch_n6(quarter, quarter)
                fetch_n6(BANK, BANK)
            else:
                for target, factor in ((s_plain, S_SCALE), (s_pair, S_SCALE * PAIR_WEIGHT)):
                    for b in range(2):
                        scale_out(target, b * BANK, BANK, factor)
                for b in range(2):
                    fetch_n5(b * BANK, BANK)
                fetch_n6(0, BANK)
                if i < PACK - 1:
                    fetch_n6(BANK, BANK)
                else:
                    fetch_n6(BANK, quarter)
                    fetch_n6(BANK + quarter, quarter)
